import numpy as np
import ml_dtypes


def mxq(x, axis, fmt="e4m3"):
    dtype, down = {"e4m3": (ml_dtypes.float8_e4m3fn, 7), "e5m2": (ml_dtypes.float8_e5m2, 14)}[fmt]
    v = np.moveaxis(np.asarray(x, np.float32).astype(ml_dtypes.bfloat16).astype(np.float64), axis, -1)
    blocks = v.reshape(v.shape[:-1] + (-1, 32))
    amax = np.abs(blocks).max(-1, keepdims=True)
    byte = np.maximum(np.where(amax > 0, np.frexp(amax)[1] - 1 + 127, 0) - down, 1)
    scale = np.exp2(byte - 127.0)
    codes = (blocks / scale).astype(np.float32).astype(dtype).astype(np.float64)
    return np.moveaxis((codes * scale).reshape(v.shape), -1, axis)


WIDE = False


def mx_kscale(k):
    if not WIDE:
        return np.ones(k)
    levels = np.array([10, -10, 5, -5, 0])
    if k % 512:
        return np.exp2(np.random.permutation(np.resize(levels, k // 32))).repeat(32)
    a = np.empty((k // 512, 16))
    for p in range(k // 512):
        a[p, :8] = np.random.permutation(np.resize(levels, 8))
        for g in range(8):
            far = levels[np.abs(levels - a[p, g]) >= 10]
            a[p, g + 8] = far[np.random.randint(len(far))]
    return np.exp2(a.ravel()).repeat(32)


def f64(x):
    return np.asarray(x).astype(np.float64)


def striped(idx):
    return np.tile(idx.reshape(-1, 16).T, (8, 1)).astype(np.uint16)


def unstriped(offs):
    return offs[:16].T.reshape(-1).astype(np.int64)


def striped8(idx):
    return np.concatenate([x.reshape(-1, 16).T for x in idx]).astype(np.uint16)


def runs(offs, k):
    lists = np.stack([offs[16 * r : 16 * r + 16].T.reshape(-1) for r in range(8)]).astype(np.int64)
    return lists[np.arange(k) % 512 // 64]


def pack_weight(w):
    k, n = w.shape
    w = f64(np.asarray(w, np.float32).astype(ml_dtypes.bfloat16)).reshape(k // 32, 32, n)
    amax = np.abs(w).max(1)
    byte = np.clip(np.where(amax > 0, np.frexp(amax)[1] - 1 + 127 - 7, 1), 1, 254)
    scaled = (w * np.exp2(127.0 - byte)[:, None, :]).reshape(k, n).astype(np.float32)
    words = np.ascontiguousarray(scaled.reshape(k // 512, 128, 4, n).transpose(0, 1, 3, 2)).astype(ml_dtypes.float8_e4m3fn).view(np.uint8)
    return words, np.ascontiguousarray(byte.astype(np.uint8).reshape(k // 512, 16, n))


def unpack_weight(words, scales):
    g, p, n, _ = words.shape
    vals = np.ascontiguousarray(words).view(ml_dtypes.float8_e4m3fn).astype(np.float64) * np.repeat(np.exp2(scales.astype(np.float64) - 127.0), 8, axis=1)[..., None]
    return vals.transpose(0, 1, 3, 2).reshape(g * 512, n)


def sigmoid(v):
    return 1.0 / (1.0 + np.exp(-np.maximum(v, -700.0)))

def planes(y):
    n, m = y.shape
    v = y.astype(np.float32).astype(ml_dtypes.bfloat16).astype(np.float64).reshape(n // 32, 32, m)
    top = np.abs(v).max(1)
    byte = np.clip(np.where(top > 0, np.frexp(top)[1] - 1 + 127 - 7, 1), 1, 254)
    codes = (v * np.exp2(127.0 - byte)[:, None, :]).reshape(n, m).astype(np.float32).astype(ml_dtypes.float8_e4m3fn).view(np.uint8)
    words = codes.reshape(n // 512, 128, 4, m).transpose(0, 1, 3, 2)
    return np.ascontiguousarray(words), np.ascontiguousarray(byte.astype(np.uint8).reshape(n // 512, 16, m))


K, T, S, N, G, H = 512, 2048, 512, 512, 2048, 512


def setup_inputs():
    n = np.random.standard_normal
    s = mx_kscale(K)[:, None]
    u = mx_kscale(S)
    packed_xT = pack_weight(n((K, T)) * s)
    packed_dT = pack_weight(n((K, G)) / s)
    packed_w1 = pack_weight(n((H, N)) / np.sqrt(2 * H) / u[:, None])
    packed_w2 = pack_weight(n((K, N)) / np.sqrt(2 * K) / s)
    return {
        "x_words": packed_xT[0],
        "x_scales": packed_xT[1],
        "d_words": packed_dT[0],
        "d_scales": packed_dT[1],
        "gn": (np.random.uniform(0.5, 1.5, (H, 1)) * u[:, None]).astype(np.float32),
        "w1_words": packed_w1[0],
        "w1_scales": packed_w1[1],
        "w2_words": packed_w2[0],
        "w2_scales": packed_w2[1],
        "offs": striped(np.random.permutation(T)[:S]),
        "k1": striped8(np.random.randint(0, G, (8, H))),
        "n1": striped(np.random.permutation(S)),
        "n2": striped(np.random.permutation(S)),
        "two": striped(np.random.permutation(T)[:S]),
        "n3": striped(np.random.permutation(S)),
        "n4": striped(np.random.permutation(S)),
    }


def reference(x_words, x_scales, d_words, d_scales, gn, w1_words, w1_scales, w2_words, w2_scales, offs, k1, n1, n2, two, n3, n4):
    d_k1 = unpack_weight(d_words, d_scales)[np.arange(K)[:, None], runs(k1, K)]
    xq = unpack_weight(x_words, x_scales)[:, unstriped(offs)]
    s = 0.0625 * (d_k1.T @ xq)
    z = f64(gn) * ((s - s[:, unstriped(n1)]) * (sigmoid(s[:, unstriped(n2)])))
    x_two = unpack_weight(x_words, x_scales)[:, unstriped(two)]
    h = unpack_weight(w1_words, w1_scales).T @ mxq(z, 0, "e4m3") + unpack_weight(w2_words, w2_scales).T @ x_two
    ex = np.exp(0.5 * h)
    out_0 = (2.0 * ex) / (ex + ex[:, unstriped(n3)] + ex[:, unstriped(n4)])
    return (out_0,) + planes(out_0)

@@ -1,0 +1,197 @@
+from contextlib import ExitStack
+
+import concourse.mybir as mybir
+
+F32 = mybir.dt.float32
+BF16 = mybir.dt.bfloat16
+U32 = mybir.dt.uint32
+I32 = mybir.dt.int32
+U16 = mybir.dt.uint16
+U8 = mybir.dt.uint8
+FP8X4 = mybir.dt.float8_e4m3fn_x4
+ACT = mybir.ActivationFunctionType
+ALU = mybir.AluOpType
+
+P = 128
+PACK = 4
+S = 512
+TABLE = 2048
+PAD = 16
+V_COPIES = 2
+PIECES = (128, 128, 128, 128)
+
+FLOPS = 3 * 2 * 512 * 512 * 512
+
+
+def tile_picked_kmixgdifshare_none_po_kernel(
+    tc, x_words, x_scales, d_words, d_scales, gn, w1_words, w1_scales, w2_words, w2_scales,
+    offs, k1, n1, n2, two, n3, n4, out_0, out_1, out_2,
+):
+    nc = tc.nc
+    with ExitStack() as ctx:
+        lists = ctx.enter_context(tc.tile_pool(name="lists", bufs=1))
+        sb = ctx.enter_context(tc.tile_pool(name="sb", bufs=1))
+        ps = ctx.enter_context(tc.psum_pool(name="ps", bufs=1))
+
+        def load_list(src, name):
+            t = lists.tile([P, S // 16], U16, name=name)
+            nc.sync.dma_start(out=t[:], in_=src)
+            return t
+
+        def words_view(w):
+            return w[0].rearrange("p n t -> p (n t)").bitcast(I32)
+
+        def deal(ap):
+            return ap.rearrange("p (m t) -> p t m", t=PACK)
+
+        d_sc = sb.tile([P, TABLE], U8, name="d_sc", align_bytes=64)
+        x_sc = sb.tile([P, TABLE], U8, name="x_sc", tag="x_then_w_sc", align_bytes=64)
+        key_sc = sb.tile([P, S], U8, name="key_sc", tag="key_then_w_sc", align_bytes=64)
+        nc.gpsimd.memset(x_sc[:].bitcast(I32), 0)
+        nc.vector.memset(key_sc[:].bitcast(I32), 0)
+
+        k1_l = load_list(k1, "k1_l")
+        nc.sync.dma_start(out=d_sc[:].bitcast(I32), in_=d_scales[0].bitcast(I32).unsqueeze(1).to_broadcast([16, 8, TABLE // 4]))
+        offs_l = load_list(offs, "offs_l")
+        gain = sb.tile([P, PACK], F32, name="gain")
+        nc.sync.dma_start(out=gain[:], in_=gn.rearrange("(p t) o -> p (t o)", t=PACK))
+        n1_l = load_list(n1, "n1_l")
+        two_l = load_list(two, "two_l")
+        d_w = sb.tile([P, TABLE], U32, name="d_w", tag="d_then_w1", align_bytes=64)
+        nc.sync.dma_start(out=d_w[:].bitcast(I32), in_=words_view(d_words))
+        x_w = sb.tile([P, TABLE], U32, name="x_w", align_bytes=64)
+        nc.sync.dma_start(out=x_w[:].bitcast(I32), in_=words_view(x_words))
+        n2_l = load_list(n2, "n2_l")
+        n3_l = load_list(n3, "n3_l")
+        n4_l = load_list(n4, "n4_l")
+        for q in range(4):
+            nc.gpsimd.dma_start(out=x_sc[32 * q:32 * q + 4, :].bitcast(I32), in_=x_scales[0, 4 * q:4 * q + 4, :].bitcast(I32))
+
+        def windows(name):
+            tiles = [sb.tile([P, S + PAD], F32, name="%s%d" % (name, t)) for t in range(PACK)]
+            for w in tiles:
+                nc.vector.memset(w[:, S:], 0.0)
+            return tiles
+
+        gs_win = windows("gs_win")
+        sig_win = windows("sig_win")
+        ex_win = windows("ex_win")
+
+        key_sc_g = sb.tile([P, S], U8, name="key_sc_g", align_bytes=64)
+        nc.vector.tensor_copy(out=key_sc_g[:], in_=d_sc[:].indirect(k1_l[:]))
+        key_sc_d = sb.tile([P, PACK, P], U8, name="key_sc_d", align_bytes=64)
+        nc.vector.tensor_copy(out=key_sc_d[:], in_=deal(key_sc_g[:]))
+        key_sc_flat = key_sc_d[:].rearrange("p t m -> p (t m)")
+        for i in range(4):
+            src = 8 * i
+            nc.scalar.dma_start(out=key_sc[i:P:32, :].bitcast(I32), in_=key_sc_flat[src:P:32, :].bitcast(I32))
+        key_w_g = sb.tile([P, S], U32, name="key_w_g", tag="key_then_w2", align_bytes=64)
+        nc.vector.tensor_copy(out=key_w_g[:], in_=d_w[:].indirect(k1_l[:]))
+        key_w = sb.tile([P, PACK, P], U32, name="key_w", align_bytes=64)
+        nc.vector.tensor_copy(out=key_w[:].bitcast(I32), in_=deal(key_w_g[:].bitcast(I32)))
+
+        w1_w = sb.tile([P, S], U32, name="w1_w", tag="d_then_w1", align_bytes=64)
+        nc.sync.dma_start(out=w1_w[:].bitcast(I32), in_=words_view(w1_words))
+        w2_w = sb.tile([P, S], U32, name="w2_w", tag="key_then_w2", align_bytes=64)
+        nc.sync.dma_start(out=w2_w[:].bitcast(I32), in_=words_view(w2_words))
+
+        def pick_tokens(lst, name):
+            sc = sb.tile([P, S], U8, name=name + "_sc", align_bytes=64)
+            nc.vector.tensor_copy(out=sc[:], in_=x_sc[:].indirect(lst[:]))
+            w = sb.tile([P, S], U32, name=name + "_w", align_bytes=64)
+            nc.vector.tensor_copy(out=w[:], in_=x_w[:].indirect(lst[:]))
+            return w, sc
+
+        tok_w, tok_sc = pick_tokens(offs_l, "tok")
+
+        gain16 = sb.tile([P, PACK], F32, name="gain16")
+        nc.vector.tensor_scalar(out=gain16[:], in0=gain[:], scalar1=0.0625, scalar2=None, op0=ALU.mult)
+
+        s_ps = [ps.tile([P, S], F32, name="s_ps%d" % t) for t in range(PACK)]
+        for t in range(PACK):
+            nc.tensor.matmul_mx(
+                out=s_ps[t][:], lhsT=key_w[:, t, :].bitcast(FP8X4), lhsT_scale=key_sc[:, t * P:(t + 1) * P],
+                rhs=tok_w[:].bitcast(FP8X4), rhs_scale=tok_sc[:], start=True, stop=True,
+            )
+
+        z = sb.tile([P, PACK, S], F32, name="z")
+        for t in range(PACK):
+            if t < V_COPIES:
+                nc.vector.tensor_scalar(out=gs_win[t][:, :S], in0=s_ps[t][:], scalar1=gain16[:, t:t + 1], scalar2=None, op0=ALU.mult)
+            else:
+                nc.scalar.activation(out=gs_win[t][:, :S], in_=s_ps[t][:], func=ACT.Copy, scale=gain16[:, t:t + 1])
+            nc.scalar.activation(out=sig_win[t][:, :S], in_=s_ps[t][:], func=ACT.Sigmoid, scale=0.0625)
+            gs_n1 = sb.tile([P, S], F32, name="gs_n1_%d" % t, tag="gs_n1_%d" % t, align_bytes=64)
+            nc.scalar.activation(out=gs_n1[:], in_=gs_win[t][:].indirect(n1_l[:]), func=ACT.Copy)
+            diff = sb.tile([P, S], F32, name="diff%d" % t)
+            nc.vector.tensor_tensor(out=diff[:], in0=gs_win[t][:, :S], in1=gs_n1[:], op=ALU.subtract)
+            nc.vector.tensor_tensor(out=z[:, t, :], in0=sig_win[t][:].indirect(n2_l[:]), in1=diff[:], op=ALU.mult)
+
+        two_w, two_sc = pick_tokens(two_l, "two")
+        w_sc = sb.tile([P, S], U8, name="w_sc", tag="x_then_w_sc", align_bytes=64)
+        nc.vector.memset(w_sc[:].bitcast(I32), 0)
+        for k, w_scales in enumerate((w1_scales, w2_scales)):
+            for q in range(4):
+                lo = 32 * q + 4 * k
+                nc.sync.dma_start(out=w_sc[lo:lo + 4, :].bitcast(I32), in_=w_scales[0, 4 * q:4 * q + 4, :].bitcast(I32))
+
+        w1_d = sb.tile([P, PACK, P], U32, name="w1_d", tag="gs_n1_2", align_bytes=64)
+        w2_d = sb.tile([P, PACK, P], U32, name="w2_d", tag="gs_n1_1", align_bytes=64)
+        nc.scalar.copy(out=w2_d[:], in_=deal(w2_w[:]))
+        nc.scalar.copy(out=w1_d[:], in_=deal(w1_w[:]))
+        w_sc_d = sb.tile([P, PACK, P], U8, name="w_sc_d", tag="key_then_w_sc", align_bytes=64)
+        nc.vector.tensor_copy(out=w_sc_d[:], in_=deal(w_sc[:]))
+
+        h_ps = [ps.tile([P, S], F32, name="h_ps%d" % t) for t in range(PACK)]
+        for t in range(PACK):
+            nc.tensor.matmul_mx(
+                out=h_ps[t][:], lhsT=w2_d[:, t, :].bitcast(FP8X4), lhsT_scale=w_sc_d[4:P, t, :],
+                rhs=two_w[:].bitcast(FP8X4), rhs_scale=two_sc[:], start=True, stop=False,
+            )
+
+        HALF = S // 2
+        for hf in range(2):
+            cols = slice(hf * HALF, (hf + 1) * HALF)
+            zb = sb.tile([P, HALF, PACK], BF16, name="zb%d" % hf, align_bytes=64)
+            nc.vector.tensor_copy(out=zb[:], in_=z[:, :, cols].rearrange("p t j -> p j t"))
+            zq_w = sb.tile([P, HALF], U32, name="zq_w%d" % hf, align_bytes=64)
+            zq_sc = sb.tile([P, HALF], U8, name="zq_sc%d" % hf, align_bytes=64)
+            nc.vector.quantize_mx(out=zq_w[:].bitcast(FP8X4), scales=zq_sc[:], in_=zb[:].rearrange("p j t -> p (j t)"))
+            for t in range(PACK):
+                nc.tensor.matmul_mx(
+                    out=h_ps[t][:, cols], lhsT=w1_d[:, t, :].bitcast(FP8X4), lhsT_scale=w_sc_d[:, t, :],
+                    rhs=zq_w[:].bitcast(FP8X4), rhs_scale=zq_sc[:], start=False, stop=(hf == 1),
+                )
+
+        den = sb.tile([P, PACK, S], F32, name="den")
+        for t in range(PACK):
+            nc.scalar.activation(out=ex_win[t][:, :S], in_=h_ps[t][:], func=ACT.Exp, scale=0.5)
+            ex_n3 = sb.tile([P, S], F32, name="ex_n3_%d" % t)
+            nc.scalar.activation(out=ex_n3[:], in_=ex_win[t][:].indirect(n3_l[:]), func=ACT.Copy)
+            others = sb.tile([P, S], F32, name="others%d" % t)
+            nc.vector.tensor_tensor(out=others[:], in0=ex_win[t][:].indirect(n4_l[:]), in1=ex_n3[:], op=ALU.add)
+            nc.vector.tensor_tensor(out=den[:, t, :], in0=others[:], in1=ex_win[t][:, :S], op=ALU.add)
+
+        out_rows = out_0.rearrange("(p t) j -> p t j", t=PACK)
+        o_w = sb.tile([P, S], U32, name="o_w", align_bytes=64)
+        o_sc = sb.tile([P, S], U8, name="o_sc", align_bytes=64)
+        out_words = words_view(out_1)
+        c0 = 0
+        for n, width in enumerate(PIECES):
+            cols = slice(c0, c0 + width)
+            c0 = c0 + width
+            root = sb.tile([P, PACK, width], F32, name="root%d" % n)
+            nc.scalar.activation(out=root[:], in_=den[:, :, cols], func=ACT.Abs_reciprocal_sqrt, scale=0.5)
+            inv = sb.tile([P, PACK, width], F32, name="inv%d" % n)
+            nc.scalar.activation(out=inv[:], in_=root[:], func=ACT.Square)
+            o = sb.tile([P, PACK, width], F32, name="o%d" % n)
+            for t in range(PACK):
+                nc.vector.tensor_tensor(out=o[:, t, :], in0=ex_win[t][:, cols], in1=inv[:, t, :], op=ALU.mult)
+            nc.sync.dma_start(out=out_rows[:, :, cols], in_=o[:])
+            ob = sb.tile([P, width, PACK], BF16, name="ob%d" % n, align_bytes=64)
+            nc.vector.tensor_copy(out=ob[:], in_=o[:].rearrange("p t j -> p j t"))
+            nc.vector.quantize_mx(out=o_w[:, cols].bitcast(FP8X4), scales=o_sc[:, cols], in_=ob[:].rearrange("p j t -> p (j t)"))
+            nc.sync.dma_start(out=out_words[:, cols], in_=o_w[:, cols].bitcast(I32))
+        for q in range(4):
+            queue = nc.sync if q % 2 else nc.scalar
+            queue.dma_start(out=out_2[0, 4 * q:4 * q + 4, :].bitcast(I32), in_=o_sc[32 * q:32 * q + 4, :].bitcast(I32))

@@ -17,8 +17,8 @@ PACK = 4
 S = 512
 TABLE = 2048
 PAD = 16
-V_COPIES = 2
-PIECES = (128, 128, 128, 128)
+PIECES = (64, 128, 128, 128, 64)
+EARLY = PIECES[0] + PIECES[1]
 
 FLOPS = 3 * 2 * 512 * 512 * 512
 
@@ -45,27 +45,29 @@ def tile_picked_kmixgdifshare_none_po_kernel(
             return ap.rearrange("p (m t) -> p t m", t=PACK)
 
         d_sc = sb.tile([P, TABLE], U8, name="d_sc", align_bytes=64)
-        x_sc = sb.tile([P, TABLE], U8, name="x_sc", tag="x_then_w_sc", align_bytes=64)
-        key_sc = sb.tile([P, S], U8, name="key_sc", tag="key_then_w_sc", align_bytes=64)
-        nc.gpsimd.memset(x_sc[:].bitcast(I32), 0)
-        nc.vector.memset(key_sc[:].bitcast(I32), 0)
+        x_sc = sb.tile([P, TABLE], U8, name="x_sc", align_bytes=64)
+        nc.vector.memset(x_sc[:].bitcast(I32), 0)
 
         k1_l = load_list(k1, "k1_l")
-        nc.sync.dma_start(out=d_sc[:].bitcast(I32), in_=d_scales[0].bitcast(I32).unsqueeze(1).to_broadcast([16, 8, TABLE // 4]))
-        offs_l = load_list(offs, "offs_l")
-        gain = sb.tile([P, PACK], F32, name="gain")
-        nc.sync.dma_start(out=gain[:], in_=gn.rearrange("(p t) o -> p (t o)", t=PACK))
-        n1_l = load_list(n1, "n1_l")
-        two_l = load_list(two, "two_l")
+        for b in range(2):
+            nc.sync.dma_start(
+                out=d_sc[b:P:2, :].bitcast(I32),
+                in_=d_scales[0, b:16:2, :].bitcast(I32).unsqueeze(1).to_broadcast([8, 8, TABLE // 4]),
+            )
         d_w = sb.tile([P, TABLE], U32, name="d_w", tag="d_then_w1", align_bytes=64)
         nc.sync.dma_start(out=d_w[:].bitcast(I32), in_=words_view(d_words))
         x_w = sb.tile([P, TABLE], U32, name="x_w", align_bytes=64)
         nc.sync.dma_start(out=x_w[:].bitcast(I32), in_=words_view(x_words))
-        n2_l = load_list(n2, "n2_l")
-        n3_l = load_list(n3, "n3_l")
-        n4_l = load_list(n4, "n4_l")
         for q in range(4):
-            nc.gpsimd.dma_start(out=x_sc[32 * q:32 * q + 4, :].bitcast(I32), in_=x_scales[0, 4 * q:4 * q + 4, :].bitcast(I32))
+            nc.scalar.dma_start(out=x_sc[32 * q:32 * q + 4, :].bitcast(I32), in_=x_scales[0, 4 * q:4 * q + 4, :].bitcast(I32))
+        offs_l = load_list(offs, "offs_l")
+        two_l = load_list(two, "two_l")
+        gain = sb.tile([P, PACK], F32, name="gain")
+        nc.sync.dma_start(out=gain[:], in_=gn.rearrange("(p t) o -> p (t o)", t=PACK))
+        n1_l = load_list(n1, "n1_l")
+        n2_l = load_list(n2, "n2_l")
+        n4_l = load_list(n4, "n4_l")
+        n3_l = load_list(n3, "n3_l")
 
         def windows(name):
             tiles = [sb.tile([P, S + PAD], F32, name="%s%d" % (name, t)) for t in range(PACK)]
@@ -77,14 +79,12 @@ def tile_picked_kmixgdifshare_none_po_kernel(
         sig_win = windows("sig_win")
         ex_win = windows("ex_win")
 
-        key_sc_g = sb.tile([P, S], U8, name="key_sc_g", align_bytes=64)
+        key_sc_g = sb.tile([P, S], U8, name="key_sc_g", tag="picked_then_w_sc", align_bytes=64)
         nc.vector.tensor_copy(out=key_sc_g[:], in_=d_sc[:].indirect(k1_l[:]))
-        key_sc_d = sb.tile([P, PACK, P], U8, name="key_sc_d", align_bytes=64)
-        nc.vector.tensor_copy(out=key_sc_d[:], in_=deal(key_sc_g[:]))
-        key_sc_flat = key_sc_d[:].rearrange("p t m -> p (t m)")
-        for i in range(4):
-            src = 8 * i
-            nc.scalar.dma_start(out=key_sc[i:P:32, :].bitcast(I32), in_=key_sc_flat[src:P:32, :].bitcast(I32))
+        key_sc = sb.tile([P, S], U8, name="key_sc", tag="key_then_w_sc", align_bytes=64)
+        nc.vector.tensor_copy(out=key_sc[:].rearrange("p (t m) -> p t m", t=PACK), in_=deal(key_sc_g[:]))
+        for b in range(2):
+            nc.scalar.dma_start(out=key_sc[2 + b:P:32, :].bitcast(I32), in_=key_sc[16 + b:P:32, :].bitcast(I32))
         key_w_g = sb.tile([P, S], U32, name="key_w_g", tag="key_then_w2", align_bytes=64)
         nc.vector.tensor_copy(out=key_w_g[:], in_=d_w[:].indirect(k1_l[:]))
         key_w = sb.tile([P, PACK, P], U32, name="key_w", align_bytes=64)
@@ -94,6 +94,13 @@ def tile_picked_kmixgdifshare_none_po_kernel(
         nc.sync.dma_start(out=w1_w[:].bitcast(I32), in_=words_view(w1_words))
         w2_w = sb.tile([P, S], U32, name="w2_w", tag="key_then_w2", align_bytes=64)
         nc.sync.dma_start(out=w2_w[:].bitcast(I32), in_=words_view(w2_words))
+
+        w_sc = sb.tile([P, S], U8, name="w_sc", tag="picked_then_w_sc", align_bytes=64)
+        nc.gpsimd.memset(w_sc[:].bitcast(I32), 0)
+        for k, w_scales in enumerate((w1_scales, w2_scales)):
+            for q in range(4):
+                lo = 32 * q + 4 * k
+                nc.sync.dma_start(out=w_sc[lo:lo + 4, :].bitcast(I32), in_=w_scales[0, 4 * q:4 * q + 4, :].bitcast(I32))
 
         def pick_tokens(lst, name):
             sc = sb.tile([P, S], U8, name=name + "_sc", align_bytes=64)
@@ -114,33 +121,33 @@ def tile_picked_kmixgdifshare_none_po_kernel(
                 rhs=tok_w[:].bitcast(FP8X4), rhs_scale=tok_sc[:], start=True, stop=True,
             )
 
+        two_w, two_sc = pick_tokens(two_l, "two")
+
         z = sb.tile([P, PACK, S], F32, name="z")
+
         for t in range(PACK):
-            if t < V_COPIES:
+            if t > 0:
                 nc.vector.tensor_scalar(out=gs_win[t][:, :S], in0=s_ps[t][:], scalar1=gain16[:, t:t + 1], scalar2=None, op0=ALU.mult)
-            else:
-                nc.scalar.activation(out=gs_win[t][:, :S], in_=s_ps[t][:], func=ACT.Copy, scale=gain16[:, t:t + 1])
             nc.scalar.activation(out=sig_win[t][:, :S], in_=s_ps[t][:], func=ACT.Sigmoid, scale=0.0625)
-            gs_n1 = sb.tile([P, S], F32, name="gs_n1_%d" % t, tag="gs_n1_%d" % t, align_bytes=64)
+            if t == 0:
+                nc.scalar.activation(out=gs_win[t][:, :S], in_=s_ps[t][:], func=ACT.Copy, scale=gain16[:, t:t + 1])
+            gs_n1 = sb.tile([P, S], F32, name="gs_n1_%d" % t)
             nc.scalar.activation(out=gs_n1[:], in_=gs_win[t][:].indirect(n1_l[:]), func=ACT.Copy)
             diff = sb.tile([P, S], F32, name="diff%d" % t)
             nc.vector.tensor_tensor(out=diff[:], in0=gs_win[t][:, :S], in1=gs_n1[:], op=ALU.subtract)
-            nc.vector.tensor_tensor(out=z[:, t, :], in0=sig_win[t][:].indirect(n2_l[:]), in1=diff[:], op=ALU.mult)
+            if t < PACK - 1:
+                nc.vector.tensor_tensor(out=z[:, t, :], in0=sig_win[t][:].indirect(n2_l[:]), in1=diff[:], op=ALU.mult)
+            else:
+                sig_n2 = sb.tile([P, S], F32, name="sig_n2")
+                nc.scalar.activation(out=sig_n2[:], in_=sig_win[t][:].indirect(n2_l[:]), func=ACT.Copy)
+                nc.vector.tensor_tensor(out=z[:, t, :], in0=sig_n2[:], in1=diff[:], op=ALU.mult)
 
-        two_w, two_sc = pick_tokens(two_l, "two")
-        w_sc = sb.tile([P, S], U8, name="w_sc", tag="x_then_w_sc", align_bytes=64)
-        nc.vector.memset(w_sc[:].bitcast(I32), 0)
-        for k, w_scales in enumerate((w1_scales, w2_scales)):
-            for q in range(4):
-                lo = 32 * q + 4 * k
-                nc.sync.dma_start(out=w_sc[lo:lo + 4, :].bitcast(I32), in_=w_scales[0, 4 * q:4 * q + 4, :].bitcast(I32))
-
-        w1_d = sb.tile([P, PACK, P], U32, name="w1_d", tag="gs_n1_2", align_bytes=64)
-        w2_d = sb.tile([P, PACK, P], U32, name="w2_d", tag="gs_n1_1", align_bytes=64)
-        nc.scalar.copy(out=w2_d[:], in_=deal(w2_w[:]))
-        nc.scalar.copy(out=w1_d[:], in_=deal(w1_w[:]))
-        w_sc_d = sb.tile([P, PACK, P], U8, name="w_sc_d", tag="key_then_w_sc", align_bytes=64)
-        nc.vector.tensor_copy(out=w_sc_d[:], in_=deal(w_sc[:]))
+        w_sc_d = sb.tile([P, PACK, P], U8, name="w_sc_d", align_bytes=64)
+        nc.gpsimd.tensor_copy(out=w_sc_d[:], in_=deal(w_sc[:]))
+        w1_d = sb.tile([P, PACK, P], U32, name="w1_d", align_bytes=64)
+        w2_d = sb.tile([P, PACK, P], U32, name="w2_d", align_bytes=64)
+        nc.gpsimd.tensor_copy(out=w2_d[:], in_=deal(w2_w[:]))
+        nc.gpsimd.tensor_copy(out=w1_d[:], in_=deal(w1_w[:]))
 
         h_ps = [ps.tile([P, S], F32, name="h_ps%d" % t) for t in range(PACK)]
         for t in range(PACK):
@@ -150,6 +157,7 @@ def tile_picked_kmixgdifshare_none_po_kernel(
             )
 
         HALF = S // 2
+        zq = []
         for hf in range(2):
             cols = slice(hf * HALF, (hf + 1) * HALF)
             zb = sb.tile([P, HALF, PACK], BF16, name="zb%d" % hf, align_bytes=64)
@@ -157,41 +165,53 @@ def tile_picked_kmixgdifshare_none_po_kernel(
             zq_w = sb.tile([P, HALF], U32, name="zq_w%d" % hf, align_bytes=64)
             zq_sc = sb.tile([P, HALF], U8, name="zq_sc%d" % hf, align_bytes=64)
             nc.vector.quantize_mx(out=zq_w[:].bitcast(FP8X4), scales=zq_sc[:], in_=zb[:].rearrange("p j t -> p (j t)"))
-            for t in range(PACK):
+            zq.append((cols, zq_w, zq_sc))
+        for t in range(PACK):
+            for hf, (cols, zq_w, zq_sc) in enumerate(zq):
                 nc.tensor.matmul_mx(
                     out=h_ps[t][:, cols], lhsT=w1_d[:, t, :].bitcast(FP8X4), lhsT_scale=w_sc_d[:, t, :],
                     rhs=zq_w[:].bitcast(FP8X4), rhs_scale=zq_sc[:], start=False, stop=(hf == 1),
                 )
 
+        ex = sb.tile([P, PACK, S], F32, name="ex")
         den = sb.tile([P, PACK, S], F32, name="den")
         for t in range(PACK):
             nc.scalar.activation(out=ex_win[t][:, :S], in_=h_ps[t][:], func=ACT.Exp, scale=0.5)
             ex_n3 = sb.tile([P, S], F32, name="ex_n3_%d" % t)
             nc.scalar.activation(out=ex_n3[:], in_=ex_win[t][:].indirect(n3_l[:]), func=ACT.Copy)
-            others = sb.tile([P, S], F32, name="others%d" % t)
-            nc.vector.tensor_tensor(out=others[:], in0=ex_win[t][:].indirect(n4_l[:]), in1=ex_n3[:], op=ALU.add)
-            nc.vector.tensor_tensor(out=den[:, t, :], in0=others[:], in1=ex_win[t][:, :S], op=ALU.add)
+            nc.vector.tensor_copy(out=ex[:, t, :], in_=ex_win[t][:, :S])
+            pair = sb.tile([P, S], F32, name="pair%d" % t)
+            cuts = (0, S) if t < PACK - 1 else (0, EARLY, S)
+            for lo, hi in zip(cuts, cuts[1:]):
+                nc.vector.tensor_tensor(
+                    out=pair[:, lo:hi], in0=ex_win[t][:].indirect(n4_l[:, lo // 16:hi // 16]), in1=ex[:, t, lo:hi], op=ALU.add,
+                )
+                nc.vector.tensor_tensor(out=den[:, t, lo:hi], in0=pair[:, lo:hi], in1=ex_n3[:, lo:hi], op=ALU.add)
 
         out_rows = out_0.rearrange("(p t) j -> p t j", t=PACK)
         o_w = sb.tile([P, S], U32, name="o_w", align_bytes=64)
         o_sc = sb.tile([P, S], U8, name="o_sc", align_bytes=64)
         out_words = words_view(out_1)
         c0 = 0
+        stored = 0
         for n, width in enumerate(PIECES):
             cols = slice(c0, c0 + width)
-            c0 = c0 + width
+            c0 = cols.stop
+            last = n == len(PIECES) - 1
             root = sb.tile([P, PACK, width], F32, name="root%d" % n)
             nc.scalar.activation(out=root[:], in_=den[:, :, cols], func=ACT.Abs_reciprocal_sqrt, scale=0.5)
             inv = sb.tile([P, PACK, width], F32, name="inv%d" % n)
             nc.scalar.activation(out=inv[:], in_=root[:], func=ACT.Square)
             o = sb.tile([P, PACK, width], F32, name="o%d" % n)
-            for t in range(PACK):
-                nc.vector.tensor_tensor(out=o[:, t, :], in0=ex_win[t][:, cols], in1=inv[:, t, :], op=ALU.mult)
-            nc.sync.dma_start(out=out_rows[:, :, cols], in_=o[:])
+            nc.vector.tensor_tensor(out=o[:], in0=ex[:, :, cols], in1=inv[:], op=ALU.mult)
+            queue = nc.scalar if last else nc.sync
+            queue.dma_start(out=out_rows[:, :, cols], in_=o[:])
             ob = sb.tile([P, width, PACK], BF16, name="ob%d" % n, align_bytes=64)
             nc.vector.tensor_copy(out=ob[:], in_=o[:].rearrange("p t j -> p j t"))
             nc.vector.quantize_mx(out=o_w[:, cols].bitcast(FP8X4), scales=o_sc[:, cols], in_=ob[:].rearrange("p j t -> p (j t)"))
-            nc.sync.dma_start(out=out_words[:, cols], in_=o_w[:, cols].bitcast(I32))
+            if last or n == 2:
+                nc.sync.dma_start(out=out_words[:, stored:c0], in_=o_w[:, stored:c0].bitcast(I32))
+                stored = c0
         for q in range(4):
             queue = nc.sync if q % 2 else nc.scalar
             queue.dma_start(out=out_2[0, 4 * q:4 * q + 4, :].bitcast(I32), in_=o_sc[32 * q:32 * q + 4, :].bitcast(I32))

@@ -41,6 +41,11 @@ def tile_picked_kmixgdifshare_none_po_kernel(
         def words_view(w):
             return w[0].rearrange("p n t -> p (n t)").bitcast(I32)
 
+        def weave(dst, src):
+            nc.vector.tensor_copy(
+                out=dst.rearrange("p (c i) t -> p c t i", i=PACK), in_=src.rearrange("p t (c i) -> p c t i", i=PACK),
+            )
+
         def deal(ap):
             return ap.rearrange("p (m t) -> p t m", t=PACK)
 
@@ -69,15 +74,15 @@ def tile_picked_kmixgdifshare_none_po_kernel(
         n4_l = load_list(n4, "n4_l")
         n3_l = load_list(n3, "n3_l")
 
-        def windows(name):
-            tiles = [sb.tile([P, S + PAD], F32, name="%s%d" % (name, t)) for t in range(PACK)]
+        def windows(name, count):
+            tiles = [sb.tile([P, S + PAD], F32, name="%s%d" % (name, t)) for t in range(count)]
             for w in tiles:
                 nc.vector.memset(w[:, S:], 0.0)
             return tiles
 
-        gs_win = windows("gs_win")
-        sig_win = windows("sig_win")
-        ex_win = windows("ex_win")
+        s_win = windows("s_win", PACK)
+        sig_win = windows("sig_win", 1)[0]
+        ex_win = windows("ex_win", PACK)
 
         key_sc_g = sb.tile([P, S], U8, name="key_sc_g", tag="picked_then_w_sc", align_bytes=64)
         nc.vector.tensor_copy(out=key_sc_g[:], in_=d_sc[:].indirect(k1_l[:]))
@@ -111,8 +116,8 @@ def tile_picked_kmixgdifshare_none_po_kernel(
 
         tok_w, tok_sc = pick_tokens(offs_l, "tok")
 
-        gain16 = sb.tile([P, PACK], F32, name="gain16")
-        nc.vector.tensor_scalar(out=gain16[:], in0=gain[:], scalar1=0.0625, scalar2=None, op0=ALU.mult)
+        gain16 = sb.tile([P, 1], F32, name="gain16")
+        nc.vector.tensor_scalar(out=gain16[:], in0=gain[:, 0:1], scalar1=0.0625, scalar2=None, op0=ALU.mult)
 
         s_ps = [ps.tile([P, S], F32, name="s_ps%d" % t) for t in range(PACK)]
         for t in range(PACK):
@@ -123,24 +128,30 @@ def tile_picked_kmixgdifshare_none_po_kernel(
 
         two_w, two_sc = pick_tokens(two_l, "two")
 
-        z = sb.tile([P, PACK, S], F32, name="z")
 
+        HALF = S // 2
+        halves = [slice(0, HALF), slice(HALF, S)]
+        z = [sb.tile([P, PACK, HALF], F32, name="z%d" % hf) for hf in range(2)]
         for t in range(PACK):
-            if t > 0:
-                nc.vector.tensor_scalar(out=gs_win[t][:, :S], in0=s_ps[t][:], scalar1=gain16[:, t:t + 1], scalar2=None, op0=ALU.mult)
-            nc.scalar.activation(out=sig_win[t][:, :S], in_=s_ps[t][:], func=ACT.Sigmoid, scale=0.0625)
-            if t == 0:
-                nc.scalar.activation(out=gs_win[t][:, :S], in_=s_ps[t][:], func=ACT.Copy, scale=gain16[:, t:t + 1])
-            gs_n1 = sb.tile([P, S], F32, name="gs_n1_%d" % t)
-            nc.scalar.activation(out=gs_n1[:], in_=gs_win[t][:].indirect(n1_l[:]), func=ACT.Copy)
+            s_n1 = sb.tile([P, S], F32, name="s_n1_%d" % t)
             diff = sb.tile([P, S], F32, name="diff%d" % t)
-            nc.vector.tensor_tensor(out=diff[:], in0=gs_win[t][:, :S], in1=gs_n1[:], op=ALU.subtract)
-            if t < PACK - 1:
-                nc.vector.tensor_tensor(out=z[:, t, :], in0=sig_win[t][:].indirect(n2_l[:]), in1=diff[:], op=ALU.mult)
+            if t == 0:
+                nc.scalar.activation(out=sig_win[:, :S], in_=s_ps[t][:], func=ACT.Sigmoid, scale=0.0625)
+                nc.scalar.activation(out=s_win[t][:, :S], in_=s_ps[t][:], func=ACT.Copy, scale=gain16[:])
             else:
-                sig_n2 = sb.tile([P, S], F32, name="sig_n2")
-                nc.scalar.activation(out=sig_n2[:], in_=sig_win[t][:].indirect(n2_l[:]), func=ACT.Copy)
-                nc.vector.tensor_tensor(out=z[:, t, :], in0=sig_n2[:], in1=diff[:], op=ALU.mult)
+                nc.vector.tensor_scalar(out=s_win[t][:, :S], in0=s_ps[t][:], scalar1=0.0625, scalar2=None, op0=ALU.mult)
+            nc.scalar.activation(out=s_n1[:], in_=s_win[t][:].indirect(n1_l[:]), func=ACT.Copy)
+            nc.vector.tensor_tensor(out=diff[:], in0=s_win[t][:, :S], in1=s_n1[:], op=ALU.subtract)
+            for hf, cols in enumerate(halves):
+                n2_half = n2_l[:, cols.start // 16:cols.stop // 16]
+                if t == 0:
+                    nc.vector.tensor_tensor(out=z[hf][:, t, :], in0=sig_win[:].indirect(n2_half), in1=diff[:, cols], op=ALU.mult)
+                else:
+                    sig_n2 = sb.tile([P, HALF], F32, name="sig_n2_%d_%d" % (t, hf))
+                    nc.scalar.activation(out=sig_n2[:], in_=s_win[t][:].indirect(n2_half), func=ACT.Sigmoid)
+                    nc.vector.scalar_tensor_tensor(
+                        out=z[hf][:, t, :], in0=diff[:, cols], scalar=gain[:, t:t + 1], in1=sig_n2[:], op0=ALU.mult, op1=ALU.mult,
+                    )
 
         w_sc_d = sb.tile([P, PACK, P], U8, name="w_sc_d", align_bytes=64)
         nc.gpsimd.tensor_copy(out=w_sc_d[:], in_=deal(w_sc[:]))
@@ -156,21 +167,17 @@ def tile_picked_kmixgdifshare_none_po_kernel(
                 rhs=two_w[:].bitcast(FP8X4), rhs_scale=two_sc[:], start=True, stop=False,
             )
 
-        HALF = S // 2
-        zq = []
-        for hf in range(2):
-            cols = slice(hf * HALF, (hf + 1) * HALF)
+        zq_w = sb.tile([P, S], U32, name="zq_w", align_bytes=64)
+        zq_sc = sb.tile([P, S], U8, name="zq_sc", align_bytes=64)
+        for hf, cols in enumerate(halves):
             zb = sb.tile([P, HALF, PACK], BF16, name="zb%d" % hf, align_bytes=64)
-            nc.vector.tensor_copy(out=zb[:], in_=z[:, :, cols].rearrange("p t j -> p j t"))
-            zq_w = sb.tile([P, HALF], U32, name="zq_w%d" % hf, align_bytes=64)
-            zq_sc = sb.tile([P, HALF], U8, name="zq_sc%d" % hf, align_bytes=64)
-            nc.vector.quantize_mx(out=zq_w[:].bitcast(FP8X4), scales=zq_sc[:], in_=zb[:].rearrange("p j t -> p (j t)"))
-            zq.append((cols, zq_w, zq_sc))
+            weave(zb[:], z[hf][:])
+            nc.vector.quantize_mx(out=zq_w[:, cols].bitcast(FP8X4), scales=zq_sc[:, cols], in_=zb[:].rearrange("p j t -> p (j t)"))
         for t in range(PACK):
-            for hf, (cols, zq_w, zq_sc) in enumerate(zq):
+            for cols in halves if t == 0 else [slice(0, S)]:
                 nc.tensor.matmul_mx(
                     out=h_ps[t][:, cols], lhsT=w1_d[:, t, :].bitcast(FP8X4), lhsT_scale=w_sc_d[:, t, :],
-                    rhs=zq_w[:].bitcast(FP8X4), rhs_scale=zq_sc[:], start=False, stop=(hf == 1),
+                    rhs=zq_w[:, cols].bitcast(FP8X4), rhs_scale=zq_sc[:, cols], start=False, stop=(cols.stop == S),
                 )
 
         ex = sb.tile([P, PACK, S], F32, name="ex")
@@ -207,7 +214,7 @@ def tile_picked_kmixgdifshare_none_po_kernel(
             queue = nc.scalar if last else nc.sync
             queue.dma_start(out=out_rows[:, :, cols], in_=o[:])
             ob = sb.tile([P, width, PACK], BF16, name="ob%d" % n, align_bytes=64)
-            nc.vector.tensor_copy(out=ob[:], in_=o[:].rearrange("p t j -> p j t"))
+            weave(ob[:], o[:])
             nc.vector.quantize_mx(out=o_w[:, cols].bitcast(FP8X4), scales=o_sc[:, cols], in_=ob[:].rearrange("p j t -> p (j t)"))
             if last or n == 2:
                 nc.sync.dma_start(out=out_words[:, stored:c0], in_=o_w[:, stored:c0].bitcast(I32))

@@ -17,6 +17,8 @@ PACK = 4
 S = 512
 TABLE = 2048
 PAD = 16
+V_FETCHED = 2
+HALF = S // 2
 PIECES = (64, 128, 128, 128, 64)
 EARLY = PIECES[0] + PIECES[1]
 
@@ -41,13 +43,15 @@ def tile_picked_kmixgdifshare_none_po_kernel(
         def words_view(w):
             return w[0].rearrange("p n t -> p (n t)").bitcast(I32)
 
-        def weave(dst, src):
-            nc.vector.tensor_copy(
+        def weave(dst, src, copy):
+            copy(
                 out=dst.rearrange("p (c i) t -> p c t i", i=PACK), in_=src.rearrange("p t (c i) -> p c t i", i=PACK),
             )
 
         def deal(ap):
             return ap.rearrange("p (m t) -> p t m", t=PACK)
+
+        halves = [slice(0, HALF), slice(HALF, S)]
 
         d_sc = sb.tile([P, TABLE], U8, name="d_sc", align_bytes=64)
         x_sc = sb.tile([P, TABLE], U8, name="x_sc", align_bytes=64)
@@ -81,7 +85,7 @@ def tile_picked_kmixgdifshare_none_po_kernel(
             return tiles
 
         s_win = windows("s_win", PACK)
-        sig_win = windows("sig_win", 1)[0]
+        sig_win = windows("sig_win", V_FETCHED)
         ex_win = windows("ex_win", PACK)
 
         key_sc_g = sb.tile([P, S], U8, name="key_sc_g", tag="picked_then_w_sc", align_bytes=64)
@@ -107,45 +111,48 @@ def tile_picked_kmixgdifshare_none_po_kernel(
                 lo = 32 * q + 4 * k
                 nc.sync.dma_start(out=w_sc[lo:lo + 4, :].bitcast(I32), in_=w_scales[0, 4 * q:4 * q + 4, :].bitcast(I32))
 
-        def pick_tokens(lst, name):
+        def pick_tokens(lst, name, cuts):
             sc = sb.tile([P, S], U8, name=name + "_sc", align_bytes=64)
             nc.vector.tensor_copy(out=sc[:], in_=x_sc[:].indirect(lst[:]))
             w = sb.tile([P, S], U32, name=name + "_w", align_bytes=64)
-            nc.vector.tensor_copy(out=w[:], in_=x_w[:].indirect(lst[:]))
+            for cols in cuts:
+                nc.vector.tensor_copy(out=w[:, cols], in_=x_w[:].indirect(lst[:, cols.start // 16:cols.stop // 16]))
             return w, sc
 
-        tok_w, tok_sc = pick_tokens(offs_l, "tok")
+        tok_w, tok_sc = pick_tokens(offs_l, "tok", halves)
 
-        gain16 = sb.tile([P, 1], F32, name="gain16")
-        nc.vector.tensor_scalar(out=gain16[:], in0=gain[:, 0:1], scalar1=0.0625, scalar2=None, op0=ALU.mult)
+        gain16 = sb.tile([P, V_FETCHED], F32, name="gain16")
+        nc.vector.tensor_scalar(out=gain16[:], in0=gain[:, :V_FETCHED], scalar1=0.0625, scalar2=None, op0=ALU.mult)
 
         s_ps = [ps.tile([P, S], F32, name="s_ps%d" % t) for t in range(PACK)]
         for t in range(PACK):
-            nc.tensor.matmul_mx(
-                out=s_ps[t][:], lhsT=key_w[:, t, :].bitcast(FP8X4), lhsT_scale=key_sc[:, t * P:(t + 1) * P],
-                rhs=tok_w[:].bitcast(FP8X4), rhs_scale=tok_sc[:], start=True, stop=True,
-            )
+            for cols in halves if t == 0 else [slice(0, S)]:
+                nc.tensor.matmul_mx(
+                    out=s_ps[t][:, cols], lhsT=key_w[:, t, :].bitcast(FP8X4), lhsT_scale=key_sc[:, t * P:(t + 1) * P],
+                    rhs=tok_w[:, cols].bitcast(FP8X4), rhs_scale=tok_sc[:, cols], start=True, stop=True,
+                )
 
-        two_w, two_sc = pick_tokens(two_l, "two")
+        two_w, two_sc = pick_tokens(two_l, "two", [slice(0, S)])
 
 
-        HALF = S // 2
-        halves = [slice(0, HALF), slice(HALF, S)]
         z = [sb.tile([P, PACK, HALF], F32, name="z%d" % hf) for hf in range(2)]
         for t in range(PACK):
             s_n1 = sb.tile([P, S], F32, name="s_n1_%d" % t)
             diff = sb.tile([P, S], F32, name="diff%d" % t)
             if t == 0:
-                nc.scalar.activation(out=sig_win[:, :S], in_=s_ps[t][:], func=ACT.Sigmoid, scale=0.0625)
-                nc.scalar.activation(out=s_win[t][:, :S], in_=s_ps[t][:], func=ACT.Copy, scale=gain16[:])
+                nc.scalar.activation(out=sig_win[t][:, :S], in_=s_ps[t][:], func=ACT.Sigmoid, scale=0.0625)
+                nc.scalar.activation(out=s_win[t][:, :S], in_=s_ps[t][:], func=ACT.Copy, scale=gain16[:, t:t + 1])
             else:
-                nc.vector.tensor_scalar(out=s_win[t][:, :S], in0=s_ps[t][:], scalar1=0.0625, scalar2=None, op0=ALU.mult)
+                factor = gain16[:, t:t + 1] if t < V_FETCHED else 0.0625
+                nc.vector.tensor_scalar(out=s_win[t][:, :S], in0=s_ps[t][:], scalar1=factor, scalar2=None, op0=ALU.mult)
+                if t < V_FETCHED:
+                    nc.scalar.activation(out=sig_win[t][:, :S], in_=s_ps[t][:], func=ACT.Sigmoid, scale=0.0625)
             nc.scalar.activation(out=s_n1[:], in_=s_win[t][:].indirect(n1_l[:]), func=ACT.Copy)
             nc.vector.tensor_tensor(out=diff[:], in0=s_win[t][:, :S], in1=s_n1[:], op=ALU.subtract)
             for hf, cols in enumerate(halves):
                 n2_half = n2_l[:, cols.start // 16:cols.stop // 16]
-                if t == 0:
-                    nc.vector.tensor_tensor(out=z[hf][:, t, :], in0=sig_win[:].indirect(n2_half), in1=diff[:, cols], op=ALU.mult)
+                if t < V_FETCHED:
+                    nc.vector.tensor_tensor(out=z[hf][:, t, :], in0=sig_win[t][:].indirect(n2_half), in1=diff[:, cols], op=ALU.mult)
                 else:
                     sig_n2 = sb.tile([P, HALF], F32, name="sig_n2_%d_%d" % (t, hf))
                     nc.scalar.activation(out=sig_n2[:], in_=s_win[t][:].indirect(n2_half), func=ACT.Sigmoid)
@@ -171,7 +178,7 @@ def tile_picked_kmixgdifshare_none_po_kernel(
         zq_sc = sb.tile([P, S], U8, name="zq_sc", align_bytes=64)
         for hf, cols in enumerate(halves):
             zb = sb.tile([P, HALF, PACK], BF16, name="zb%d" % hf, align_bytes=64)
-            weave(zb[:], z[hf][:])
+            weave(zb[:], z[hf][:], nc.vector.tensor_copy)
             nc.vector.quantize_mx(out=zq_w[:, cols].bitcast(FP8X4), scales=zq_sc[:, cols], in_=zb[:].rearrange("p j t -> p (j t)"))
         for t in range(PACK):
             for cols in halves if t == 0 else [slice(0, S)]:
@@ -214,7 +221,7 @@ def tile_picked_kmixgdifshare_none_po_kernel(
             queue = nc.scalar if last else nc.sync
             queue.dma_start(out=out_rows[:, :, cols], in_=o[:])
             ob = sb.tile([P, width, PACK], BF16, name="ob%d" % n, align_bytes=64)
-            weave(ob[:], o[:])
+            weave(ob[:], o[:], nc.scalar.copy if n == len(PIECES) - 2 else nc.vector.tensor_copy)
             nc.vector.quantize_mx(out=o_w[:, cols].bitcast(FP8X4), scales=o_sc[:, cols], in_=ob[:].rearrange("p j t -> p (j t)"))
             if last or n == 2:
                 nc.sync.dma_start(out=out_words[:, stored:c0], in_=o_w[:, stored:c0].bitcast(I32))

from contextlib import ExitStack

import concourse.mybir as mybir

F32 = mybir.dt.float32
BF16 = mybir.dt.bfloat16
U32 = mybir.dt.uint32
I32 = mybir.dt.int32
U16 = mybir.dt.uint16
U8 = mybir.dt.uint8
FP8X4 = mybir.dt.float8_e4m3fn_x4
ACT = mybir.ActivationFunctionType
ALU = mybir.AluOpType

P = 128
PACK = 4
S = 512
TABLE = 2048
PAD = 16
V_FETCHED = 2
HALF = S // 2
PIECES = (64, 128, 128, 128, 64)
EARLY = PIECES[0] + PIECES[1]

FLOPS = 3 * 2 * 512 * 512 * 512


def tile_picked_kmixgdifshare_none_po_kernel(
    tc, x_words, x_scales, d_words, d_scales, gn, w1_words, w1_scales, w2_words, w2_scales,
    offs, k1, n1, n2, two, n3, n4, out_0, out_1, out_2,
):
    nc = tc.nc
    with ExitStack() as ctx:
        lists = ctx.enter_context(tc.tile_pool(name="lists", bufs=1))
        sb = ctx.enter_context(tc.tile_pool(name="sb", bufs=1))
        ps = ctx.enter_context(tc.psum_pool(name="ps", bufs=1))

        def load_list(src, name):
            t = lists.tile([P, S // 16], U16, name=name)
            nc.sync.dma_start(out=t[:], in_=src)
            return t

        def words_view(w):
            return w[0].rearrange("p n t -> p (n t)").bitcast(I32)

        def weave(dst, src, copy):
            copy(
                out=dst.rearrange("p (c i) t -> p c t i", i=PACK), in_=src.rearrange("p t (c i) -> p c t i", i=PACK),
            )

        def deal(ap):
            return ap.rearrange("p (m t) -> p t m", t=PACK)

        halves = [slice(0, HALF), slice(HALF, S)]

        d_sc = sb.tile([P, TABLE], U8, name="d_sc", align_bytes=64)
        x_sc = sb.tile([P, TABLE], U8, name="x_sc", align_bytes=64)
        nc.vector.memset(x_sc[:].bitcast(I32), 0)

        k1_l = load_list(k1, "k1_l")
        for b in range(2):
            nc.sync.dma_start(
                out=d_sc[b:P:2, :].bitcast(I32),
                in_=d_scales[0, b:16:2, :].bitcast(I32).unsqueeze(1).to_broadcast([8, 8, TABLE // 4]),
            )
        d_w = sb.tile([P, TABLE], U32, name="d_w", tag="d_then_w1", align_bytes=64)
        nc.sync.dma_start(out=d_w[:].bitcast(I32), in_=words_view(d_words))
        x_w = sb.tile([P, TABLE], U32, name="x_w", align_bytes=64)
        nc.sync.dma_start(out=x_w[:].bitcast(I32), in_=words_view(x_words))
        for q in range(4):
            nc.scalar.dma_start(out=x_sc[32 * q:32 * q + 4, :].bitcast(I32), in_=x_scales[0, 4 * q:4 * q + 4, :].bitcast(I32))
        offs_l = load_list(offs, "offs_l")
        two_l = load_list(two, "two_l")
        gain = sb.tile([P, PACK], F32, name="gain")
        nc.sync.dma_start(out=gain[:], in_=gn.rearrange("(p t) o -> p (t o)", t=PACK))
        n1_l = load_list(n1, "n1_l")
        n2_l = load_list(n2, "n2_l")
        n4_l = load_list(n4, "n4_l")
        n3_l = load_list(n3, "n3_l")

        def windows(name, count):
            tiles = [sb.tile([P, S + PAD], F32, name="%s%d" % (name, t)) for t in range(count)]
            for w in tiles:
                nc.vector.memset(w[:, S:], 0.0)
            return tiles

        s_win = windows("s_win", PACK)
        sig_win = windows("sig_win", V_FETCHED)
        ex_win = windows("ex_win", PACK)

        key_sc_g = sb.tile([P, S], U8, name="key_sc_g", tag="picked_then_w_sc", align_bytes=64)
        nc.vector.tensor_copy(out=key_sc_g[:], in_=d_sc[:].indirect(k1_l[:]))
        key_sc = sb.tile([P, S], U8, name="key_sc", tag="key_then_w_sc", align_bytes=64)
        nc.vector.tensor_copy(out=key_sc[:].rearrange("p (t m) -> p t m", t=PACK), in_=deal(key_sc_g[:]))
        for b in range(2):
            nc.scalar.dma_start(out=key_sc[2 + b:P:32, :].bitcast(I32), in_=key_sc[16 + b:P:32, :].bitcast(I32))
        key_w_g = sb.tile([P, S], U32, name="key_w_g", tag="key_then_w2", align_bytes=64)
        nc.vector.tensor_copy(out=key_w_g[:], in_=d_w[:].indirect(k1_l[:]))
        key_w = sb.tile([P, PACK, P], U32, name="key_w", align_bytes=64)
        nc.vector.tensor_copy(out=key_w[:].bitcast(I32), in_=deal(key_w_g[:].bitcast(I32)))

        w1_w = sb.tile([P, S], U32, name="w1_w", tag="d_then_w1", align_bytes=64)
        nc.sync.dma_start(out=w1_w[:].bitcast(I32), in_=words_view(w1_words))
        w2_w = sb.tile([P, S], U32, name="w2_w", tag="key_then_w2", align_bytes=64)
        nc.sync.dma_start(out=w2_w[:].bitcast(I32), in_=words_view(w2_words))

        w_sc = sb.tile([P, S], U8, name="w_sc", tag="picked_then_w_sc", align_bytes=64)
        nc.gpsimd.memset(w_sc[:].bitcast(I32), 0)
        for k, w_scales in enumerate((w1_scales, w2_scales)):
            for q in range(4):
                lo = 32 * q + 4 * k
                nc.sync.dma_start(out=w_sc[lo:lo + 4, :].bitcast(I32), in_=w_scales[0, 4 * q:4 * q + 4, :].bitcast(I32))

        def pick_tokens(lst, name, cuts):
            sc = sb.tile([P, S], U8, name=name + "_sc", align_bytes=64)
            nc.vector.tensor_copy(out=sc[:], in_=x_sc[:].indirect(lst[:]))
            w = sb.tile([P, S], U32, name=name + "_w", align_bytes=64)
            for cols in cuts:
                nc.vector.tensor_copy(out=w[:, cols], in_=x_w[:].indirect(lst[:, cols.start // 16:cols.stop // 16]))
            return w, sc

        tok_w, tok_sc = pick_tokens(offs_l, "tok", halves)

        gain16 = sb.tile([P, V_FETCHED], F32, name="gain16")
        nc.vector.tensor_scalar(out=gain16[:], in0=gain[:, :V_FETCHED], scalar1=0.0625, scalar2=None, op0=ALU.mult)

        s_ps = [ps.tile([P, S], F32, name="s_ps%d" % t) for t in range(PACK)]
        for t in range(PACK):
            for cols in halves if t == 0 else [slice(0, S)]:
                nc.tensor.matmul_mx(
                    out=s_ps[t][:, cols], lhsT=key_w[:, t, :].bitcast(FP8X4), lhsT_scale=key_sc[:, t * P:(t + 1) * P],
                    rhs=tok_w[:, cols].bitcast(FP8X4), rhs_scale=tok_sc[:, cols], start=True, stop=True,
                )

        two_w, two_sc = pick_tokens(two_l, "two", [slice(0, S)])


        z = [sb.tile([P, PACK, HALF], F32, name="z%d" % hf) for hf in range(2)]
        for t in range(PACK):
            s_n1 = sb.tile([P, S], F32, name="s_n1_%d" % t)
            diff = sb.tile([P, S], F32, name="diff%d" % t)
            if t == 0:
                nc.scalar.activation(out=sig_win[t][:, :S], in_=s_ps[t][:], func=ACT.Sigmoid, scale=0.0625)
                nc.scalar.activation(out=s_win[t][:, :S], in_=s_ps[t][:], func=ACT.Copy, scale=gain16[:, t:t + 1])
            else:
                factor = gain16[:, t:t + 1] if t < V_FETCHED else 0.0625
                nc.vector.tensor_scalar(out=s_win[t][:, :S], in0=s_ps[t][:], scalar1=factor, scalar2=None, op0=ALU.mult)
                if t < V_FETCHED:
                    nc.scalar.activation(out=sig_win[t][:, :S], in_=s_ps[t][:], func=ACT.Sigmoid, scale=0.0625)
            nc.scalar.activation(out=s_n1[:], in_=s_win[t][:].indirect(n1_l[:]), func=ACT.Copy)
            nc.vector.tensor_tensor(out=diff[:], in0=s_win[t][:, :S], in1=s_n1[:], op=ALU.subtract)
            for hf, cols in enumerate(halves):
                n2_half = n2_l[:, cols.start // 16:cols.stop // 16]
                if t < V_FETCHED:
                    nc.vector.tensor_tensor(out=z[hf][:, t, :], in0=sig_win[t][:].indirect(n2_half), in1=diff[:, cols], op=ALU.mult)
                else:
                    sig_n2 = sb.tile([P, HALF], F32, name="sig_n2_%d_%d" % (t, hf))
                    nc.scalar.activation(out=sig_n2[:], in_=s_win[t][:].indirect(n2_half), func=ACT.Sigmoid)
                    nc.vector.scalar_tensor_tensor(
                        out=z[hf][:, t, :], in0=diff[:, cols], scalar=gain[:, t:t + 1], in1=sig_n2[:], op0=ALU.mult, op1=ALU.mult,
                    )

        w_sc_d = sb.tile([P, PACK, P], U8, name="w_sc_d", align_bytes=64)
        nc.gpsimd.tensor_copy(out=w_sc_d[:], in_=deal(w_sc[:]))
        w1_d = sb.tile([P, PACK, P], U32, name="w1_d", align_bytes=64)
        w2_d = sb.tile([P, PACK, P], U32, name="w2_d", align_bytes=64)
        nc.gpsimd.tensor_copy(out=w2_d[:], in_=deal(w2_w[:]))
        nc.gpsimd.tensor_copy(out=w1_d[:], in_=deal(w1_w[:]))

        h_ps = [ps.tile([P, S], F32, name="h_ps%d" % t) for t in range(PACK)]
        for t in range(PACK):
            nc.tensor.matmul_mx(
                out=h_ps[t][:], lhsT=w2_d[:, t, :].bitcast(FP8X4), lhsT_scale=w_sc_d[4:P, t, :],
                rhs=two_w[:].bitcast(FP8X4), rhs_scale=two_sc[:], start=True, stop=False,
            )

        zq_w = sb.tile([P, S], U32, name="zq_w", align_bytes=64)
        zq_sc = sb.tile([P, S], U8, name="zq_sc", align_bytes=64)
        for hf, cols in enumerate(halves):
            zb = sb.tile([P, HALF, PACK], BF16, name="zb%d" % hf, align_bytes=64)
            weave(zb[:], z[hf][:], nc.vector.tensor_copy)
            nc.vector.quantize_mx(out=zq_w[:, cols].bitcast(FP8X4), scales=zq_sc[:, cols], in_=zb[:].rearrange("p j t -> p (j t)"))
        for t in range(PACK):
            for cols in halves if t == 0 else [slice(0, S)]:
                nc.tensor.matmul_mx(
                    out=h_ps[t][:, cols], lhsT=w1_d[:, t, :].bitcast(FP8X4), lhsT_scale=w_sc_d[:, t, :],
                    rhs=zq_w[:, cols].bitcast(FP8X4), rhs_scale=zq_sc[:, cols], start=False, stop=(cols.stop == S),
                )

        ex = sb.tile([P, PACK, S], F32, name="ex")
        den = sb.tile([P, PACK, S], F32, name="den")
        for t in range(PACK):
            nc.scalar.activation(out=ex_win[t][:, :S], in_=h_ps[t][:], func=ACT.Exp, scale=0.5)
            ex_n3 = sb.tile([P, S], F32, name="ex_n3_%d" % t)
            nc.scalar.activation(out=ex_n3[:], in_=ex_win[t][:].indirect(n3_l[:]), func=ACT.Copy)
            nc.vector.tensor_copy(out=ex[:, t, :], in_=ex_win[t][:, :S])
            pair = sb.tile([P, S], F32, name="pair%d" % t)
            cuts = (0, S) if t < PACK - 1 else (0, EARLY, S)
            for lo, hi in zip(cuts, cuts[1:]):
                nc.vector.tensor_tensor(
                    out=pair[:, lo:hi], in0=ex_win[t][:].indirect(n4_l[:, lo // 16:hi // 16]), in1=ex[:, t, lo:hi], op=ALU.add,
                )
                nc.vector.tensor_tensor(out=den[:, t, lo:hi], in0=pair[:, lo:hi], in1=ex_n3[:, lo:hi], op=ALU.add)

        out_rows = out_0.rearrange("(p t) j -> p t j", t=PACK)
        o_w = sb.tile([P, S], U32, name="o_w", align_bytes=64)
        o_sc = sb.tile([P, S], U8, name="o_sc", align_bytes=64)
        out_words = words_view(out_1)
        c0 = 0
        stored = 0
        for n, width in enumerate(PIECES):
            cols = slice(c0, c0 + width)
            c0 = cols.stop
            last = n == len(PIECES) - 1
            root = sb.tile([P, PACK, width], F32, name="root%d" % n)
            nc.scalar.activation(out=root[:], in_=den[:, :, cols], func=ACT.Abs_reciprocal_sqrt, scale=0.5)
            inv = sb.tile([P, PACK, width], F32, name="inv%d" % n)
            nc.scalar.activation(out=inv[:], in_=root[:], func=ACT.Square)
            o = sb.tile([P, PACK, width], F32, name="o%d" % n)
            nc.vector.tensor_tensor(out=o[:], in0=ex[:, :, cols], in1=inv[:], op=ALU.mult)
            queue = nc.scalar if last else nc.sync
            queue.dma_start(out=out_rows[:, :, cols], in_=o[:])
            ob = sb.tile([P, width, PACK], BF16, name="ob%d" % n, align_bytes=64)
            weave(ob[:], o[:], nc.scalar.copy if n == len(PIECES) - 2 else nc.vector.tensor_copy)
            nc.vector.quantize_mx(out=o_w[:, cols].bitcast(FP8X4), scales=o_sc[:, cols], in_=ob[:].rearrange("p j t -> p (j t)"))
            if last or n == 2:
                nc.sync.dma_start(out=out_words[:, stored:c0], in_=o_w[:, stored:c0].bitcast(I32))
                stored = c0
        for q in range(4):
            queue = nc.sync if q % 2 else nc.scalar
            queue.dma_start(out=out_2[0, 4 * q:4 * q + 4, :].bitcast(I32), in_=o_sc[32 * q:32 * q + 4, :].bitcast(I32))
